import numpy as np, ml_dtypes
CORES = [8,11,14,16,19,22,24,27,30]
N = 9
import mx_ref
NC = 128
BF = ml_dtypes.bfloat16
def setup_inputs(rng):
    def f(*shape):
        return mx_ref.flush((rng.standard_normal(shape, dtype=np.float32) * np.exp2(rng.integers(-2, 3, shape[:-1] + (1,)))).astype(BF))
    return {"w": f(N, 128, 512), "x": f(N, 128, N * 4 * NC)}
def setup_inputs_blocks(rng):
    d = setup_inputs(rng)
    for k in ("w", "x"): d[k] = mx_ref.spread(d[k], rng, 2)
    return d
def setup_inputs_wide(rng):
    d = setup_inputs(rng)
    for k in ("w", "x"): d[k] = mx_ref.flush((d[k].astype(np.float32) * np.exp2(rng.integers(-8, 9, (N, 1, 1))).astype(np.float32)).astype(BF))
    return d
def setup_inputs_zeros(rng):
    d = setup_inputs(rng); v = d["x"].reshape(N, 128, -1, 4).copy()
    v[np.broadcast_to((rng.random((N, 1, v.shape[2], 1)) < 0.33), v.shape)] = 0
    d["x"] = v.reshape(d["x"].shape)
    return d
def reference(w, x):
    QW = [mx_ref.quantize(w[j]) for j in range(N)]
    y = np.zeros((N, 128, NC), np.float32)
    for r in range(N):
        for j in range(N):
            p = mx_ref.matmul(QW[j], mx_ref.quantize(x[j][:, 4 * NC * r:4 * NC * r + 4 * NC]))
            y[r] = p if j == 0 else y[r] + p
    return {"y": y}

@@ -1,0 +1,213 @@
+from concourse.bass import DstId, RemoteDMATransfer
+from concourse.mybir import dt
+
+N = 9
+TW = 128
+NSIM = 32
+SLOTS = 36
+
+SCRATCH = {
+    "wt": ("sbuf", [128, 4 * TW], "bfloat16"),
+    "xt": ("sbuf", [128, 4 * TW * N], "bfloat16"),
+    "q": ("sbuf", [128, TW * SLOTS], "float8_e4m3fn_x4"),
+    "s": ("sbuf", [128, TW * SLOTS], "uint8"),
+    "acc": ("psum", [128, 512], "float32"),
+    "yo": ("sbuf", [128, TW], "float32"),
+}
+SEMAPHORES = ["ldw", "ld0", "ld1", "ld2", "q0", "q1", "q2", "sent", "mm", "cp", "st"] + ["a%d" % j for j in range(N)]
+
+DETOUR = True
+
+
+def _bits(m):
+    return [e for e in range(m.bit_length()) if (m >> e) & 1]
+
+
+def make_plan(cores, topo):
+    rank = {c: i for i, c in enumerate(cores)}
+    every = list(range(NSIM))
+    chips = []
+    for c in cores:
+        if topo.chip(c) not in chips:
+            chips.append(topo.chip(c))
+    allchips = sorted({topo.chip(c) for c in every})
+    on = {ch: [c for c in cores if topo.chip(c) == ch] for ch in chips}
+    free = {ch: [c for c in every if topo.chip(c) == ch and c not in rank] for ch in allchips}
+    top = {c: 0 for c in every}
+    cnt = {}
+    tasks = {c: [] for c in every}
+    groups = {c: [] for c in cores}
+    mms = {c: [] for c in cores}
+    busy_die = {}
+
+    def take(c, n):
+        a = top[c]
+        top[c] += n
+        return a
+
+    def engines(c):
+        near = [d for d in every if d != c and topo.chip(d) == topo.chip(c)][0]
+        far = [d for d in every if topo.chip(d) != topo.chip(c)][0]
+        lo = _bits(topo.mask(c, far))
+        hi = [e for e in _bits(topo.mask(c, near)) if e not in lo]
+        return lo, hi
+
+    def xfer(dst, src_slot, dst_slot, n, eng, sem):
+        cnt[(dst, sem)] = cnt.get((dst, sem), 0) + 2 * len(eng)
+        return (dst, src_slot, dst_slot, n, eng, sem)
+
+    def pick(pool, s, finals):
+        ok = [h for h in pool if all(topo.may_write(h, f) for f in finals)]
+        ok.sort(key=lambda h: (busy_die.get((topo.chip(h), topo.die(h)), 0), topo.die(h) != topo.die(s), h))
+        h = ok[0]
+        pool.remove(h)
+        busy_die[(topo.chip(h), topo.die(h))] = busy_die.get((topo.chip(h), topo.die(h)), 0) + 1
+        return h
+
+    flows = {s: [] for s in cores}
+    for s in cores:
+        A = topo.chip(s)
+        for B in chips:
+            if B == A:
+                continue
+            finals = on[B]
+            gate = finals[on[A].index(s)]
+            allowed = topo.may_write(s, gate)
+            two = not topo.mates(A, B) and not topo.same_plane(A, B)
+            mid = None
+            if two and DETOUR:
+                own_way = [C for C in allchips if topo.mates(A, C)]
+                other_way = [C for C in allchips if topo.same_plane(A, C) and topo.mates(C, B)]
+                crowded = sum(1 for c in on[A] if topo.die(c) == topo.die(s)) > 1
+                if own_way[0] in chips and other_way and other_way[0] not in chips and (crowded or not allowed):
+                    mid = pick(free[other_way[0]], s, finals)
+                    key = (0, 0)
+            if mid is None and allowed:
+                mid = gate
+                key = (1, 0) if two else ((2, 0) if topo.mates(A, B) else (3, 0))
+            if mid is None:
+                mid = pick(free[A], s, finals)
+                key = (0, 1)
+            flows[s].append((key, B, mid, two))
+        flows[s].sort()
+
+    for s in cores:
+        A = topo.chip(s)
+        j = rank[s]
+        sem = "a%d" % j
+        lo, hi = engines(s)
+        for idx, (key, B, mid, two) in enumerate(flows[s]):
+            finals = on[B]
+            mlo, mhi = engines(mid)
+            t0 = 10 + 3 * idx + (1 if two else 0)
+            if mid in finals:
+                o = [r for r in finals if r != mid]
+                base, land = take(s, 4), take(mid, 4)
+                groups[s].append((B, [(base, mid), (base + 1, o[0]), (base + 2, "W"), (base + 3, o[1])]))
+                tasks[s].append((0, (idx,), "q%d" % idx, 4, [[xfer(mid, base, land, 4, lo, sem)]]))
+                mms[mid].append((t0, land + 2, land, sem, None))
+                l0, l1 = take(o[0], 2), take(o[1], 2)
+                tasks[mid].append((1, (idx, two), sem, None,
+                                   [[xfer(o[0], land + 1, l0, 2, mlo, sem), xfer(o[1], land + 2, l1, 2, mhi, sem)]]))
+                mms[o[0]].append((t0 + 5, l0 + 1, l0, sem, None))
+                mms[o[1]].append((t0 + 5, l1, l1 + 1, sem, None))
+            else:
+                base, land = take(s, 5), take(mid, 5)
+                groups[s].append((B, [(base, finals[0]), (base + 1, "W"), (base + 2, finals[1]), (base + 3, "W"),
+                                      (base + 4, finals[2])]))
+                tasks[s].append((0, (idx,), "q%d" % idx, 5,
+                                 [[xfer(mid, base, land, 5, hi if topo.chip(mid) == A else lo, sem)]]))
+                h = len(mlo) // 2
+                l = [take(f, 2) for f in finals]
+                tasks[mid].append((1, (idx, two), sem, None,
+                                   [[xfer(finals[0], land, l[0], 2, mlo[:h], sem),
+                                     xfer(finals[1], land + 1, l[1], 2, mlo[h:], sem)],
+                                    [xfer(finals[2], land + 3, l[2], 2, mlo, sem)]]))
+                mms[finals[0]].append((t0 + 8, l[0] + 1, l[0], sem, None))
+                mms[finals[1]].append((t0 + 8, l[1], l[1] + 1, sem, None))
+                mms[finals[2]].append((t0 + 10, l[2], l[2] + 1, sem, None))
+        idx = len(flows[s])
+        p = [r for r in on[A] if r != s]
+        base = take(s, 4)
+        groups[s].append((A, [(base, p[0]), (base + 1, "W"), (base + 2, p[1]), (base + 3, s)]))
+        h = len(hi) // 2
+        l0, l1 = take(p[0], 2), take(p[1], 2)
+        tasks[s].append((0, (idx,), "q%d" % idx, 4,
+                         [[xfer(p[0], base, l0, 2, hi[:h], sem), xfer(p[1], base + 1, l1, 2, hi[h:], sem)]]))
+        mms[p[0]].append((1, l0 + 1, l0, sem, None))
+        mms[p[1]].append((1, l1, l1 + 1, sem, None))
+        mms[s].append((0, base + 1, base + 3, "q%d" % idx, 4))
+    return {"rank": rank, "on": on, "tasks": tasks, "groups": groups, "mms": mms, "cnt": cnt, "top": top}
+
+
+def rank_program(g, core, T, topo):
+    cores = list(T.cores)
+    P = make_plan(cores, topo)
+    rank, cnt = P["rank"], P["cnt"]
+    tasks = sorted(P["tasks"][core], key=lambda t: (t[0], t[1]))
+    if core not in rank and not tasks:
+        return
+
+    def cols(slot, n=1):
+        return slice(TW * slot, TW * (slot + n))
+
+    if core in rank:
+        grp = P["groups"][core]
+        g.sync.dma_start(T.wt[:], T.w[:]).then_inc(T.sem.ldw, 16)
+        for k, (ch, _) in enumerate(grp):
+            rs = [rank[c] for c in P["on"][ch]]
+            a, b = 4 * TW * min(rs), 4 * TW * (max(rs) + 1)
+            qu = g.scalar if k % 2 == 0 else g.sync
+            qu.dma_start(T.xt[:, a:b], T.x[:, a:b]).then_inc(T.sem["ld%d" % k], 16)
+        v = g.vector
+        v.wait_ge(T.sem.ldw, 16)
+        for k, (_, lay) in enumerate(grp):
+            for slot, t in lay:
+                if t == "W":
+                    v.quantize_mx(T.q[:, cols(slot)], T.s[:, cols(slot)], T.wt[:]).then_inc(T.sem["q%d" % k], 1)
+        for k, (_, lay) in enumerate(grp):
+            v.wait_ge(T.sem["ld%d" % k], 16)
+            for slot, t in lay:
+                if t != "W":
+                    r = rank[t]
+                    v.quantize_mx(T.q[:, cols(slot)], T.s[:, cols(slot)],
+                                  T.xt[:, 4 * TW * r:4 * TW * (r + 1)]).then_inc(T.sem["q%d" % k], 1)
+
+    sent = 0
+    for level, key, sem, count, calls in tasks:
+        g.wait_ge(T.sem[sem], count if count is not None else cnt[(core, sem)])
+        for group in calls:
+            for codes in (True, False):
+                trs = []
+                for dst, a, b, n, eng, rsem in group:
+                    rid, pid, _ = topo.addr(dst)
+                    m = sum(1 << e for e in eng)
+                    if codes:
+                        src, out = T.q[:, cols(a, n)].bitcast(dt.uint8), T.q[:, cols(b, n)].bitcast(dt.uint8)
+                    else:
+                        src, out = T.s[:, cols(a, n)], T.s[:, cols(b, n)]
+                    trs.append((out, src, T.sem[rsem], pid, rid, m))
+                    sent += len(eng)
+                if len(trs) == 1:
+                    out, src, rs, pid, rid, m = trs[0]
+                    g.remote_dma(out_ap=out, in_ap=src, remote_sem=rs, local_sem=T.sem.sent, pid=pid, routing_id=rid,
+                                 dma_engine_mask=m)
+                else:
+                    g.remote_dma_fused([RemoteDMATransfer(dst_ids=[DstId(rid=rid, pnc=pid)], dma_engine_mask=m,
+                                                          remote_sem=rs, src=src, dst=out)
+                                        for out, src, rs, pid, rid, m in trs], local_sem=T.sem.sent)
+    if sent:
+        g.wait_ge(T.sem.sent, sent)
+
+    if core in rank:
+        mm = sorted(P["mms"][core])
+        for i, (_, w, x, sem, count) in enumerate(mm):
+            g.tensor.wait_ge(T.sem[sem], count if count is not None else cnt[(core, sem)])
+            ins = g.tensor.matmul_mx(T.acc[:, 0:TW], T.q[:, cols(w)], T.s[:, cols(w)], T.q[:, cols(x)], T.s[:, cols(x)],
+                                     i == 0, i == len(mm) - 1)
+        ins.then_inc(T.sem.mm, 1)
+        g.vector.wait_ge(T.sem.mm, 1)
+        g.vector.tensor_copy(T.yo[:], T.acc[:, 0:TW]).then_inc(T.sem.cp, 1)
+        g.sync.wait_ge(T.sem.cp, 1)
+        g.sync.dma_start(T.y[:], T.yo[:]).then_inc(T.sem.st, 16)
+        g.sync.wait_ge(T.sem.st, 16)

@@ -14,7 +14,8 @@ SCRATCH = {
     "acc": ("psum", [128, 512], "float32"),
     "yo": ("sbuf", [128, TW], "float32"),
 }
-SEMAPHORES = ["ldw", "ld0", "ld1", "ld2", "q0", "q1", "q2", "sent", "mm", "cp", "st"] + ["a%d" % j for j in range(N)]
+SEMAPHORES = (["ldw", "ld0", "ld1", "ld2", "qw", "sent", "mm", "cp", "st"] + ["p%d" % k for k in range(5)]
+              + ["a%d" % j for j in range(N)] + ["b%d" % j for j in range(N)])
 
 DETOUR = True
 
@@ -36,7 +37,8 @@ def make_plan(cores, topo):
     top = {c: 0 for c in every}
     cnt = {}
     tasks = {c: [] for c in every}
-    groups = {c: [] for c in cores}
+    loads = {c: [] for c in cores}
+    runs = {c: [] for c in cores}
     mms = {c: [] for c in cores}
     busy_die = {}
 
@@ -56,12 +58,12 @@ def make_plan(cores, topo):
         cnt[(dst, sem)] = cnt.get((dst, sem), 0) + 2 * len(eng)
         return (dst, src_slot, dst_slot, n, eng, sem)
 
-    def pick(pool, s, finals):
+    def pick(pool, s, finals, tiles):
         ok = [h for h in pool if all(topo.may_write(h, f) for f in finals)]
         ok.sort(key=lambda h: (busy_die.get((topo.chip(h), topo.die(h)), 0), topo.die(h) != topo.die(s), h))
         h = ok[0]
         pool.remove(h)
-        busy_die[(topo.chip(h), topo.die(h))] = busy_die.get((topo.chip(h), topo.die(h)), 0) + 1
+        busy_die[(topo.chip(h), topo.die(h))] = busy_die.get((topo.chip(h), topo.die(h)), 0) + tiles
         return h
 
     flows = {s: [] for s in cores}
@@ -80,64 +82,85 @@ def make_plan(cores, topo):
                 other_way = [C for C in allchips if topo.same_plane(A, C) and topo.mates(C, B)]
                 crowded = sum(1 for c in on[A] if topo.die(c) == topo.die(s)) > 1
                 if own_way[0] in chips and other_way and other_way[0] not in chips and (crowded or not allowed):
-                    mid = pick(free[other_way[0]], s, finals)
+                    mid = (pick(free[other_way[0]], s, finals, 4), pick(free[other_way[0]], s, finals, 2))
                     key = (0, 0)
             if mid is None and allowed:
                 mid = gate
                 key = (1, 0) if two else ((2, 0) if topo.mates(A, B) else (3, 0))
             if mid is None:
-                mid = pick(free[A], s, finals)
+                mid = (pick(free[A], s, finals, 4), pick(free[A], s, finals, 2))
                 key = (0, 1)
             flows[s].append((key, B, mid, two))
-        flows[s].sort()
+        flows[s].sort(key=lambda f: f[:2])
 
     for s in cores:
         A = topo.chip(s)
         j = rank[s]
-        sem = "a%d" % j
+        sem, semb = "a%d" % j, "b%d" % j
         lo, hi = engines(s)
+        np_ = [0]
+
+        def run(piece, tiles):
+            name = "p%d" % np_[0]
+            np_[0] += 1
+            runs[s].append((name, piece, tiles))
+            return name, len(tiles)
+
+        behind = 0
         for idx, (key, B, mid, two) in enumerate(flows[s]):
             finals = on[B]
-            mlo, mhi = engines(mid)
-            t0 = 10 + 3 * idx + (1 if two else 0)
+            loads[s].append(B)
             if mid in finals:
+                mlo, mhi = engines(mid)
                 o = [r for r in finals if r != mid]
-                base, land = take(s, 4), take(mid, 4)
-                groups[s].append((B, [(base, mid), (base + 1, o[0]), (base + 2, "W"), (base + 3, o[1])]))
-                tasks[s].append((0, (idx,), "q%d" % idx, 4, [[xfer(mid, base, land, 4, lo, sem)]]))
-                mms[mid].append((t0, land + 2, land, sem, None))
+                base, la, lb = take(s, 4), take(mid, 3), take(mid, 1)
+                nm, n = run(idx, [(base, o[0]), (base + 1, "W"), (base + 2, o[1])])
+                tasks[s].append((0, (0, idx, 0), nm, n, [[xfer(mid, base, la, 3, lo, semb)]]))
+                nm, n = run(idx, [(base + 3, mid)])
+                tasks[s].append((0, (1, idx, 0), nm, n, [[xfer(mid, base + 3, lb, 1, lo, sem)]]))
+                mms[mid].append((8 + idx, la + 1, lb, [(semb, None), (sem, None)]))
                 l0, l1 = take(o[0], 2), take(o[1], 2)
-                tasks[mid].append((1, (idx, two), sem, None,
-                                   [[xfer(o[0], land + 1, l0, 2, mlo, sem), xfer(o[1], land + 2, l1, 2, mhi, sem)]]))
-                mms[o[0]].append((t0 + 5, l0 + 1, l0, sem, None))
-                mms[o[1]].append((t0 + 5, l1, l1 + 1, sem, None))
+                tasks[mid].append((1, (idx, two), semb, None,
+                                   [[xfer(o[0], la, l0, 2, mlo, sem), xfer(o[1], la + 1, l1, 2, mhi, sem)]]))
+                behind += 3
+                mms[o[0]].append((behind + 5, l0 + 1, l0, [(sem, None)]))
+                mms[o[1]].append((behind + 5, l1, l1 + 1, [(sem, None)]))
             else:
-                base, land = take(s, 5), take(mid, 5)
-                groups[s].append((B, [(base, finals[0]), (base + 1, "W"), (base + 2, finals[1]), (base + 3, "W"),
-                                      (base + 4, finals[2])]))
-                tasks[s].append((0, (idx,), "q%d" % idx, 5,
-                                 [[xfer(mid, base, land, 5, hi if topo.chip(mid) == A else lo, sem)]]))
-                h = len(mlo) // 2
+                eng = hi if topo.chip(mid[0]) == A else lo
+                if eng is lo:
+                    behind += 5
+                base, la, lb = take(s, 5), take(mid[0], 3), take(mid[1], 2)
                 l = [take(f, 2) for f in finals]
-                tasks[mid].append((1, (idx, two), sem, None,
-                                   [[xfer(finals[0], land, l[0], 2, mlo[:h], sem),
-                                     xfer(finals[1], land + 1, l[1], 2, mlo[h:], sem)],
-                                    [xfer(finals[2], land + 3, l[2], 2, mlo, sem)]]))
-                mms[finals[0]].append((t0 + 8, l[0] + 1, l[0], sem, None))
-                mms[finals[1]].append((t0 + 8, l[1], l[1] + 1, sem, None))
-                mms[finals[2]].append((t0 + 10, l[2], l[2] + 1, sem, None))
+                nm, n = run(idx, [(base, finals[0]), (base + 1, "W"), (base + 2, finals[1])])
+                tasks[s].append((0, (0, idx, 0), nm, n, [[xfer(mid[0], base, la, 3, eng, sem)]]))
+                nm, n = run(idx, [(base + 3, "W"), (base + 4, finals[2])])
+                tasks[s].append((0, (0, idx, 1), nm, n, [[xfer(mid[1], base + 3, lb, 2, eng, sem)]]))
+                mlo = engines(mid[0])[0]
+                h = len(mlo) // 2
+                tasks[mid[0]].append((1, (idx, two), sem, None,
+                                      [[xfer(finals[0], la, l[0], 2, mlo[:h], sem),
+                                        xfer(finals[1], la + 1, l[1], 2, mlo[h:], sem)]]))
+                tasks[mid[1]].append((1, (idx, two), sem, None,
+                                      [[xfer(finals[2], lb, l[2], 2, engines(mid[1])[0], sem)]]))
+                mms[finals[0]].append((11 + 2 * idx, l[0] + 1, l[0], [(sem, None)]))
+                mms[finals[1]].append((11 + 2 * idx, l[1], l[1] + 1, [(sem, None)]))
+                mms[finals[2]].append((11 + 2 * idx, l[2], l[2] + 1, [(sem, None)]))
         idx = len(flows[s])
+        loads[s].append(A)
         p = [r for r in on[A] if r != s]
         base = take(s, 4)
-        groups[s].append((A, [(base, p[0]), (base + 1, "W"), (base + 2, p[1]), (base + 3, s)]))
+        runs[s].insert(0, ("qw", idx, [(base + 1, "W")]))
+        nm, n = run(idx, [(base, p[0]), (base + 2, p[1]), (base + 3, s)])
         h = len(hi) // 2
         l0, l1 = take(p[0], 2), take(p[1], 2)
-        tasks[s].append((0, (idx,), "q%d" % idx, 4,
-                         [[xfer(p[0], base, l0, 2, hi[:h], sem), xfer(p[1], base + 1, l1, 2, hi[h:], sem)]]))
-        mms[p[0]].append((1, l0 + 1, l0, sem, None))
-        mms[p[1]].append((1, l1, l1 + 1, sem, None))
-        mms[s].append((0, base + 1, base + 3, "q%d" % idx, 4))
-    return {"rank": rank, "on": on, "tasks": tasks, "groups": groups, "mms": mms, "cnt": cnt, "top": top}
+        tasks[s].append((-1, (0,), "qw", 1,
+                         [[xfer(p[0], base + 1, l0, 1, hi[:h], sem), xfer(p[1], base + 1, l1, 1, hi[h:], sem)]]))
+        tasks[s].append((0, (2, idx, 0), nm, n,
+                         [[xfer(p[0], base, l0 + 1, 1, hi[:h], sem), xfer(p[1], base + 2, l1 + 1, 1, hi[h:], sem)]]))
+        mms[p[0]].append((1, l0, l0 + 1, [(sem, None)]))
+        mms[p[1]].append((1, l1, l1 + 1, [(sem, None)]))
+        mms[s].append((0, base + 1, base + 3, [("qw", 1), (nm, n)]))
+    return {"rank": rank, "on": on, "tasks": tasks, "loads": loads, "runs": runs, "mms": mms, "cnt": cnt, "top": top}
 
 
 def rank_program(g, core, T, topo):
@@ -152,26 +175,26 @@ def rank_program(g, core, T, topo):
         return slice(TW * slot, TW * (slot + n))
 
     if core in rank:
-        grp = P["groups"][core]
         g.sync.dma_start(T.wt[:], T.w[:]).then_inc(T.sem.ldw, 16)
-        for k, (ch, _) in enumerate(grp):
+        for k, ch in enumerate(P["loads"][core]):
             rs = [rank[c] for c in P["on"][ch]]
             a, b = 4 * TW * min(rs), 4 * TW * (max(rs) + 1)
             qu = g.scalar if k % 2 == 0 else g.sync
             qu.dma_start(T.xt[:, a:b], T.x[:, a:b]).then_inc(T.sem["ld%d" % k], 16)
         v = g.vector
         v.wait_ge(T.sem.ldw, 16)
-        for k, (_, lay) in enumerate(grp):
-            for slot, t in lay:
+        for name, _, tiles in P["runs"][core]:
+            for slot, t in tiles:
                 if t == "W":
-                    v.quantize_mx(T.q[:, cols(slot)], T.s[:, cols(slot)], T.wt[:]).then_inc(T.sem["q%d" % k], 1)
-        for k, (_, lay) in enumerate(grp):
+                    v.quantize_mx(T.q[:, cols(slot)], T.s[:, cols(slot)], T.wt[:]).then_inc(T.sem[name], 1)
+        for k in range(len(P["loads"][core])):
             v.wait_ge(T.sem["ld%d" % k], 16)
-            for slot, t in lay:
-                if t != "W":
-                    r = rank[t]
-                    v.quantize_mx(T.q[:, cols(slot)], T.s[:, cols(slot)],
-                                  T.xt[:, 4 * TW * r:4 * TW * (r + 1)]).then_inc(T.sem["q%d" % k], 1)
+            for name, piece, tiles in P["runs"][core]:
+                for slot, t in tiles:
+                    if piece == k and t != "W":
+                        r = rank[t]
+                        v.quantize_mx(T.q[:, cols(slot)], T.s[:, cols(slot)],
+                                      T.xt[:, 4 * TW * r:4 * TW * (r + 1)]).then_inc(T.sem[name], 1)
 
     sent = 0
     for level, key, sem, count, calls in tasks:
@@ -200,9 +223,10 @@ def rank_program(g, core, T, topo):
         g.wait_ge(T.sem.sent, sent)
 
     if core in rank:
-        mm = sorted(P["mms"][core])
-        for i, (_, w, x, sem, count) in enumerate(mm):
-            g.tensor.wait_ge(T.sem[sem], count if count is not None else cnt[(core, sem)])
+        mm = sorted(P["mms"][core], key=lambda e: e[:3])
+        for i, (_, w, x, waits) in enumerate(mm):
+            for sem, count in waits:
+                g.tensor.wait_ge(T.sem[sem], count if count is not None else cnt[(core, sem)])
             ins = g.tensor.matmul_mx(T.acc[:, 0:TW], T.q[:, cols(w)], T.s[:, cols(w)], T.q[:, cols(x)], T.s[:, cols(x)],
                                      i == 0, i == len(mm) - 1)
         ins.then_inc(T.sem.mm, 1)

@@ -4,7 +4,7 @@ from concourse.mybir import dt
 N = 9
 TW = 128
 NSIM = 32
-SLOTS = 36
+SLOTS = 48
 
 SCRATCH = {
     "wt": ("sbuf", [128, 4 * TW], "bfloat16"),
@@ -14,7 +14,7 @@ SCRATCH = {
     "acc": ("psum", [128, 512], "float32"),
     "yo": ("sbuf", [128, TW], "float32"),
 }
-SEMAPHORES = (["ldw", "ld0", "ld1", "ld2", "qw", "sent", "mm", "cp", "st"] + ["p%d" % k for k in range(5)]
+SEMAPHORES = (["ldw", "ld0", "ld1", "ld2", "qw", "sent", "mm", "cp", "st"] + ["p%d" % k for k in range(6)]
               + ["a%d" % j for j in range(N)] + ["b%d" % j for j in range(N)])
 
 DETOUR = True
@@ -54,9 +54,12 @@ def make_plan(cores, topo):
         hi = [e for e in _bits(topo.mask(c, near)) if e not in lo]
         return lo, hi
 
-    def xfer(dst, src_slot, dst_slot, n, eng, sem):
-        cnt[(dst, sem)] = cnt.get((dst, sem), 0) + 2 * len(eng)
-        return (dst, src_slot, dst_slot, n, eng, sem)
+    def tr(kind, dst, src_slot, dst_slot, n, eng, sem):
+        cnt[(dst, sem)] = cnt.get((dst, sem), 0) + len(eng)
+        return (kind, dst, src_slot, dst_slot, n, tuple(eng), sem)
+
+    def pair(items):
+        return [[tr("q", *i) for i in items], [tr("s", *i) for i in items]]
 
     def pick(pool, s, finals, tiles):
         ok = [h for h in pool if all(topo.may_write(h, f) for f in finals)]
@@ -106,60 +109,74 @@ def make_plan(cores, topo):
             runs[s].append((name, piece, tiles))
             return name, len(tiles)
 
-        behind = 0
+        p = [r for r in on[A] if r != s]
+        ob = take(s, 4)
+        wslot = ob + 1
+        runs[s].append(("qw", None, [(wslot, "W")]))
+        early, last = [], []
+        ngates = sum(1 for f in flows[s] if f[2] in on[f[1]])
+        ng = 0
         for idx, (key, B, mid, two) in enumerate(flows[s]):
             finals = on[B]
             loads[s].append(B)
             if mid in finals:
                 mlo, mhi = engines(mid)
                 o = [r for r in finals if r != mid]
-                base, la, lb = take(s, 4), take(mid, 3), take(mid, 1)
+                base, la = take(s, 4), take(mid, 4)
                 nm, n = run(idx, [(base, o[0]), (base + 1, "W"), (base + 2, o[1])])
-                tasks[s].append((0, (0, idx, 0), nm, n, [[xfer(mid, base, la, 3, lo, semb)]]))
+                tasks[s].append((0, (0, idx, 0), [(nm, n)], [[tr("q", mid, base, la, 3, lo, semb)]]))
                 nm, n = run(idx, [(base + 3, mid)])
-                tasks[s].append((0, (1, idx, 0), nm, n, [[xfer(mid, base + 3, lb, 1, lo, sem)]]))
-                mms[mid].append((8 + idx, la + 1, lb, [(semb, None), (sem, None)]))
+                tasks[s].append((0, (0, idx, 1), [(nm, n)], [[tr("s", mid, base, la, 4, lo, semb)]]))
+                w = len(lo) // ngates
+                last.append(tr("q", mid, base + 3, la + 3, 1, lo[ng * w:(ng + 1) * w], sem))
+                ng += 1
+                mms[mid].append((5, la + 1, la + 3, [(semb, None), (sem, None)]))
                 l0, l1 = take(o[0], 2), take(o[1], 2)
-                tasks[mid].append((1, (idx, two), semb, None,
-                                   [[xfer(o[0], la, l0, 2, mlo, sem), xfer(o[1], la + 1, l1, 2, mhi, sem)]]))
-                behind += 3
-                mms[o[0]].append((behind + 5, l0 + 1, l0, [(sem, None)]))
-                mms[o[1]].append((behind + 5, l1, l1 + 1, [(sem, None)]))
+                tasks[mid].append((1, (idx, two), [(semb, None)],
+                                   pair([(o[0], la, l0, 2, mlo, sem), (o[1], la + 1, l1, 2, mhi, sem)])))
+                mms[o[0]].append((6 + 3 * idx, l0 + 1, l0, [(sem, None)]))
+                mms[o[1]].append((6 + 3 * idx, l1, l1 + 1, [(sem, None)]))
             else:
                 eng = hi if topo.chip(mid[0]) == A else lo
-                if eng is lo:
-                    behind += 5
-                base, la, lb = take(s, 5), take(mid[0], 3), take(mid[1], 2)
-                l = [take(f, 2) for f in finals]
-                nm, n = run(idx, [(base, finals[0]), (base + 1, "W"), (base + 2, finals[1])])
-                tasks[s].append((0, (0, idx, 0), nm, n, [[xfer(mid[0], base, la, 3, eng, sem)]]))
-                nm, n = run(idx, [(base + 3, "W"), (base + 4, finals[2])])
-                tasks[s].append((0, (0, idx, 1), nm, n, [[xfer(mid[1], base + 3, lb, 2, eng, sem)]]))
-                mlo = engines(mid[0])[0]
-                h = len(mlo) // 2
-                tasks[mid[0]].append((1, (idx, two), sem, None,
-                                      [[xfer(finals[0], la, l[0], 2, mlo[:h], sem),
-                                        xfer(finals[1], la + 1, l[1], 2, mlo[h:], sem)]]))
-                tasks[mid[1]].append((1, (idx, two), sem, None,
-                                      [[xfer(finals[2], lb, l[2], 2, engines(mid[1])[0], sem)]]))
-                mms[finals[0]].append((11 + 2 * idx, l[0] + 1, l[0], [(sem, None)]))
-                mms[finals[1]].append((11 + 2 * idx, l[1], l[1] + 1, [(sem, None)]))
-                mms[finals[2]].append((11 + 2 * idx, l[2], l[2] + 1, [(sem, None)]))
+                h = len(eng) // 2
+                base = take(s, 3)
+                wa, wb, xa, xb = take(mid[0], 1), take(mid[1], 1), take(mid[0], 2), take(mid[1], 1)
+                lw = [take(f, 1) for f in finals]
+                lx = [take(f, 1) for f in finals]
+                early += [(mid[0], wslot, wa, 1, eng[:h], semb), (mid[1], wslot, wb, 1, eng[h:], semb)]
+                nm, n = run(idx, [(base, finals[0]), (base + 1, finals[1])])
+                tasks[s].append((0, (0, idx, 0), [(nm, n)], pair([(mid[0], base, xa, 2, eng, sem)])))
+                nm, n = run(idx, [(base + 2, finals[2])])
+                tasks[s].append((0, (0, idx, 1), [(nm, n)], pair([(mid[1], base + 2, xb, 1, eng, sem)])))
+                m0, m1 = engines(mid[0])[0], engines(mid[1])[0]
+                k = len(m0) // 2
+                tasks[mid[0]].append((0, (0,), [(semb, None)], pair([(finals[0], wa, lw[0], 1, m0[:k], sem),
+                                                                     (finals[1], wa, lw[1], 1, m0[k:], sem)])))
+                tasks[mid[0]].append((1, (0,), [(sem, None)], pair([(finals[0], xa, lx[0], 1, m0[:k], sem),
+                                                                    (finals[1], xa + 1, lx[1], 1, m0[k:], sem)])))
+                tasks[mid[1]].append((0, (0,), [(semb, None)], pair([(finals[2], wb, lw[2], 1, m1, sem)])))
+                tasks[mid[1]].append((1, (0,), [(sem, None)], pair([(finals[2], xb, lx[2], 1, m1, sem)])))
+                for f, a, b in zip(finals, lw, lx):
+                    mms[f].append((4 + 3 * idx, a, b, [(sem, None)]))
+        if early:
+            tasks[s].append((-2, (0,), [("qw", 1)], pair(early)))
+        used = {e for i in early for e in i[4]}
+        rest = [e for e in lo + hi if e not in used] or hi
+        h = len(rest) // 2
+        l0, l1 = take(p[0], 4), take(p[1], 4)
+        tasks[s].append((-1, (0,), [("qw", 1)], [[tr("q", p[0], wslot, l0 + 1, 1, rest[:h], sem),
+                                                  tr("q", p[1], wslot, l1 + 1, 1, rest[h:], sem)]]))
         idx = len(flows[s])
         loads[s].append(A)
-        p = [r for r in on[A] if r != s]
-        base = take(s, 4)
-        runs[s].insert(0, ("qw", idx, [(base + 1, "W")]))
-        nm, n = run(idx, [(base, p[0]), (base + 2, p[1]), (base + 3, s)])
-        h = len(hi) // 2
-        l0, l1 = take(p[0], 2), take(p[1], 2)
-        tasks[s].append((-1, (0,), "qw", 1,
-                         [[xfer(p[0], base + 1, l0, 1, hi[:h], sem), xfer(p[1], base + 1, l1, 1, hi[h:], sem)]]))
-        tasks[s].append((0, (2, idx, 0), nm, n,
-                         [[xfer(p[0], base, l0 + 1, 1, hi[:h], sem), xfer(p[1], base + 2, l1 + 1, 1, hi[h:], sem)]]))
-        mms[p[0]].append((1, l0, l0 + 1, [(sem, None)]))
-        mms[p[1]].append((1, l1, l1 + 1, [(sem, None)]))
-        mms[s].append((0, base + 1, base + 3, [("qw", 1), (nm, n)]))
+        nm, n = run(idx, [(ob, p[0]), (ob + 2, p[1]), (ob + 3, s)])
+        e = hi if ngates else lo + hi
+        k = len(e) // 4
+        last += [tr("q", p[0], ob, l0, 1, e[:k], sem), tr("q", p[1], ob + 2, l1 + 2, 1, e[k:2 * k], sem),
+                 tr("s", p[0], ob, l0, 4, e[2 * k:3 * k], sem), tr("s", p[1], ob, l1, 4, e[3 * k:], sem)]
+        tasks[s].append((0, (2,), [(nm, n)], [last]))
+        mms[p[0]].append((1, l0 + 1, l0, [(sem, None)]))
+        mms[p[1]].append((1, l1 + 1, l1 + 2, [(sem, None)]))
+        mms[s].append((0, wslot, ob + 3, [("qw", 1), (nm, n)]))
     return {"rank": rank, "on": on, "tasks": tasks, "loads": loads, "runs": runs, "mms": mms, "cnt": cnt, "top": top}
 
 
@@ -197,28 +214,28 @@ def rank_program(g, core, T, topo):
                                       T.xt[:, 4 * TW * r:4 * TW * (r + 1)]).then_inc(T.sem[name], 1)
 
     sent = 0
-    for level, key, sem, count, calls in tasks:
-        g.wait_ge(T.sem[sem], count if count is not None else cnt[(core, sem)])
-        for group in calls:
-            for codes in (True, False):
-                trs = []
-                for dst, a, b, n, eng, rsem in group:
-                    rid, pid, _ = topo.addr(dst)
-                    m = sum(1 << e for e in eng)
-                    if codes:
-                        src, out = T.q[:, cols(a, n)].bitcast(dt.uint8), T.q[:, cols(b, n)].bitcast(dt.uint8)
-                    else:
-                        src, out = T.s[:, cols(a, n)], T.s[:, cols(b, n)]
-                    trs.append((out, src, T.sem[rsem], pid, rid, m))
-                    sent += len(eng)
-                if len(trs) == 1:
-                    out, src, rs, pid, rid, m = trs[0]
-                    g.remote_dma(out_ap=out, in_ap=src, remote_sem=rs, local_sem=T.sem.sent, pid=pid, routing_id=rid,
-                                 dma_engine_mask=m)
+    for level, key, waits, calls in tasks:
+        for sem, count in waits:
+            g.wait_ge(T.sem[sem], count if count is not None else cnt[(core, sem)])
+        for call in calls:
+            trs = []
+            for kind, dst, a, b, n, eng, rsem in call:
+                rid, pid, _ = topo.addr(dst)
+                m = sum(1 << e for e in eng)
+                if kind == "q":
+                    src, out = T.q[:, cols(a, n)].bitcast(dt.uint8), T.q[:, cols(b, n)].bitcast(dt.uint8)
                 else:
-                    g.remote_dma_fused([RemoteDMATransfer(dst_ids=[DstId(rid=rid, pnc=pid)], dma_engine_mask=m,
-                                                          remote_sem=rs, src=src, dst=out)
-                                        for out, src, rs, pid, rid, m in trs], local_sem=T.sem.sent)
+                    src, out = T.s[:, cols(a, n)], T.s[:, cols(b, n)]
+                trs.append((out, src, T.sem[rsem], pid, rid, m))
+                sent += len(eng)
+            if len(trs) == 1:
+                out, src, rs, pid, rid, m = trs[0]
+                g.remote_dma(out_ap=out, in_ap=src, remote_sem=rs, local_sem=T.sem.sent, pid=pid, routing_id=rid,
+                             dma_engine_mask=m)
+            else:
+                g.remote_dma_fused([RemoteDMATransfer(dst_ids=[DstId(rid=rid, pnc=pid)], dma_engine_mask=m,
+                                                      remote_sem=rs, src=src, dst=out)
+                                    for out, src, rs, pid, rid, m in trs], local_sem=T.sem.sent)
     if sent:
         g.wait_ge(T.sem.sent, sent)
 

from concourse.bass import DstId, RemoteDMATransfer
from concourse.mybir import dt

N = 9
TW = 128
NSIM = 32
SLOTS = 48

SCRATCH = {
    "wt": ("sbuf", [128, 4 * TW], "bfloat16"),
    "xt": ("sbuf", [128, 4 * TW * N], "bfloat16"),
    "q": ("sbuf", [128, TW * SLOTS], "float8_e4m3fn_x4"),
    "s": ("sbuf", [128, TW * SLOTS], "uint8"),
    "acc": ("psum", [128, 512], "float32"),
    "yo": ("sbuf", [128, TW], "float32"),
}
SEMAPHORES = (["ldw", "ld0", "ld1", "ld2", "qw", "sent", "mm", "cp", "st"] + ["p%d" % k for k in range(6)]
              + ["a%d" % j for j in range(N)] + ["b%d" % j for j in range(N)])

DETOUR = True


def _bits(m):
    return [e for e in range(m.bit_length()) if (m >> e) & 1]


def make_plan(cores, topo):
    rank = {c: i for i, c in enumerate(cores)}
    every = list(range(NSIM))
    chips = []
    for c in cores:
        if topo.chip(c) not in chips:
            chips.append(topo.chip(c))
    allchips = sorted({topo.chip(c) for c in every})
    on = {ch: [c for c in cores if topo.chip(c) == ch] for ch in chips}
    free = {ch: [c for c in every if topo.chip(c) == ch and c not in rank] for ch in allchips}
    top = {c: 0 for c in every}
    cnt = {}
    tasks = {c: [] for c in every}
    loads = {c: [] for c in cores}
    runs = {c: [] for c in cores}
    mms = {c: [] for c in cores}
    busy_die = {}

    def take(c, n):
        a = top[c]
        top[c] += n
        return a

    def engines(c):
        near = [d for d in every if d != c and topo.chip(d) == topo.chip(c)][0]
        far = [d for d in every if topo.chip(d) != topo.chip(c)][0]
        lo = _bits(topo.mask(c, far))
        hi = [e for e in _bits(topo.mask(c, near)) if e not in lo]
        return lo, hi

    def tr(kind, dst, src_slot, dst_slot, n, eng, sem):
        cnt[(dst, sem)] = cnt.get((dst, sem), 0) + len(eng)
        return (kind, dst, src_slot, dst_slot, n, tuple(eng), sem)

    def pair(items):
        return [[tr("q", *i) for i in items], [tr("s", *i) for i in items]]

    def pick(pool, s, finals, tiles):
        ok = [h for h in pool if all(topo.may_write(h, f) for f in finals)]
        ok.sort(key=lambda h: (busy_die.get((topo.chip(h), topo.die(h)), 0), topo.die(h) != topo.die(s), h))
        h = ok[0]
        pool.remove(h)
        busy_die[(topo.chip(h), topo.die(h))] = busy_die.get((topo.chip(h), topo.die(h)), 0) + tiles
        return h

    flows = {s: [] for s in cores}
    for s in cores:
        A = topo.chip(s)
        for B in chips:
            if B == A:
                continue
            finals = on[B]
            gate = finals[on[A].index(s)]
            allowed = topo.may_write(s, gate)
            two = not topo.mates(A, B) and not topo.same_plane(A, B)
            mid = None
            if two and DETOUR:
                own_way = [C for C in allchips if topo.mates(A, C)]
                other_way = [C for C in allchips if topo.same_plane(A, C) and topo.mates(C, B)]
                crowded = sum(1 for c in on[A] if topo.die(c) == topo.die(s)) > 1
                if own_way[0] in chips and other_way and other_way[0] not in chips and (crowded or not allowed):
                    mid = (pick(free[other_way[0]], s, finals, 4), pick(free[other_way[0]], s, finals, 2))
                    key = (0, 0)
            if mid is None and allowed:
                mid = gate
                key = (1, 0) if two else ((2, 0) if topo.mates(A, B) else (3, 0))
            if mid is None:
                mid = (pick(free[A], s, finals, 4), pick(free[A], s, finals, 2))
                key = (0, 1)
            flows[s].append((key, B, mid, two))
        flows[s].sort(key=lambda f: f[:2])

    for s in cores:
        A = topo.chip(s)
        j = rank[s]
        sem, semb = "a%d" % j, "b%d" % j
        lo, hi = engines(s)
        np_ = [0]

        def run(piece, tiles):
            name = "p%d" % np_[0]
            np_[0] += 1
            runs[s].append((name, piece, tiles))
            return name, len(tiles)

        p = [r for r in on[A] if r != s]
        ob = take(s, 4)
        wslot = ob + 1
        runs[s].append(("qw", None, [(wslot, "W")]))
        early, last = [], []
        ngates = sum(1 for f in flows[s] if f[2] in on[f[1]])
        ng = 0
        for idx, (key, B, mid, two) in enumerate(flows[s]):
            finals = on[B]
            loads[s].append(B)
            if mid in finals:
                mlo, mhi = engines(mid)
                o = [r for r in finals if r != mid]
                base, la = take(s, 4), take(mid, 4)
                nm, n = run(idx, [(base, o[0]), (base + 1, "W"), (base + 2, o[1])])
                tasks[s].append((0, (0, idx, 0), [(nm, n)], [[tr("q", mid, base, la, 3, lo, semb)]]))
                nm, n = run(idx, [(base + 3, mid)])
                tasks[s].append((0, (0, idx, 1), [(nm, n)], [[tr("s", mid, base, la, 4, lo, semb)]]))
                w = len(lo) // ngates
                last.append(tr("q", mid, base + 3, la + 3, 1, lo[ng * w:(ng + 1) * w], sem))
                ng += 1
                mms[mid].append((5, la + 1, la + 3, [(semb, None), (sem, None)]))
                l0, l1 = take(o[0], 2), take(o[1], 2)
                tasks[mid].append((1, (idx, two), [(semb, None)],
                                   pair([(o[0], la, l0, 2, mlo, sem), (o[1], la + 1, l1, 2, mhi, sem)])))
                mms[o[0]].append((6 + 3 * idx, l0 + 1, l0, [(sem, None)]))
                mms[o[1]].append((6 + 3 * idx, l1, l1 + 1, [(sem, None)]))
            else:
                eng = hi if topo.chip(mid[0]) == A else lo
                h = len(eng) // 2
                base = take(s, 3)
                wa, wb, xa, xb = take(mid[0], 1), take(mid[1], 1), take(mid[0], 2), take(mid[1], 1)
                lw = [take(f, 1) for f in finals]
                lx = [take(f, 1) for f in finals]
                early += [(mid[0], wslot, wa, 1, eng[:h], semb), (mid[1], wslot, wb, 1, eng[h:], semb)]
                nm, n = run(idx, [(base, finals[0]), (base + 1, finals[1])])
                tasks[s].append((0, (0, idx, 0), [(nm, n)], pair([(mid[0], base, xa, 2, eng, sem)])))
                nm, n = run(idx, [(base + 2, finals[2])])
                tasks[s].append((0, (0, idx, 1), [(nm, n)], pair([(mid[1], base + 2, xb, 1, eng, sem)])))
                m0, m1 = engines(mid[0])[0], engines(mid[1])[0]
                k = len(m0) // 2
                tasks[mid[0]].append((0, (0,), [(semb, None)], pair([(finals[0], wa, lw[0], 1, m0[:k], sem),
                                                                     (finals[1], wa, lw[1], 1, m0[k:], sem)])))
                tasks[mid[0]].append((1, (0,), [(sem, None)], pair([(finals[0], xa, lx[0], 1, m0[:k], sem),
                                                                    (finals[1], xa + 1, lx[1], 1, m0[k:], sem)])))
                tasks[mid[1]].append((0, (0,), [(semb, None)], pair([(finals[2], wb, lw[2], 1, m1, sem)])))
                tasks[mid[1]].append((1, (0,), [(sem, None)], pair([(finals[2], xb, lx[2], 1, m1, sem)])))
                for f, a, b in zip(finals, lw, lx):
                    mms[f].append((4 + 3 * idx, a, b, [(sem, None)]))
        if early:
            tasks[s].append((-2, (0,), [("qw", 1)], pair(early)))
        used = {e for i in early for e in i[4]}
        rest = [e for e in lo + hi if e not in used] or hi
        h = len(rest) // 2
        l0, l1 = take(p[0], 4), take(p[1], 4)
        tasks[s].append((-1, (0,), [("qw", 1)], [[tr("q", p[0], wslot, l0 + 1, 1, rest[:h], sem),
                                                  tr("q", p[1], wslot, l1 + 1, 1, rest[h:], sem)]]))
        idx = len(flows[s])
        loads[s].append(A)
        nm, n = run(idx, [(ob, p[0]), (ob + 2, p[1]), (ob + 3, s)])
        e = hi if ngates else lo + hi
        k = len(e) // 4
        last += [tr("q", p[0], ob, l0, 1, e[:k], sem), tr("q", p[1], ob + 2, l1 + 2, 1, e[k:2 * k], sem),
                 tr("s", p[0], ob, l0, 4, e[2 * k:3 * k], sem), tr("s", p[1], ob, l1, 4, e[3 * k:], sem)]
        tasks[s].append((0, (2,), [(nm, n)], [last]))
        mms[p[0]].append((1, l0 + 1, l0, [(sem, None)]))
        mms[p[1]].append((1, l1 + 1, l1 + 2, [(sem, None)]))
        mms[s].append((0, wslot, ob + 3, [("qw", 1), (nm, n)]))
    return {"rank": rank, "on": on, "tasks": tasks, "loads": loads, "runs": runs, "mms": mms, "cnt": cnt, "top": top}


def rank_program(g, core, T, topo):
    cores = list(T.cores)
    P = make_plan(cores, topo)
    rank, cnt = P["rank"], P["cnt"]
    tasks = sorted(P["tasks"][core], key=lambda t: (t[0], t[1]))
    if core not in rank and not tasks:
        return

    def cols(slot, n=1):
        return slice(TW * slot, TW * (slot + n))

    if core in rank:
        g.sync.dma_start(T.wt[:], T.w[:]).then_inc(T.sem.ldw, 16)
        for k, ch in enumerate(P["loads"][core]):
            rs = [rank[c] for c in P["on"][ch]]
            a, b = 4 * TW * min(rs), 4 * TW * (max(rs) + 1)
            qu = g.scalar if k % 2 == 0 else g.sync
            qu.dma_start(T.xt[:, a:b], T.x[:, a:b]).then_inc(T.sem["ld%d" % k], 16)
        v = g.vector
        v.wait_ge(T.sem.ldw, 16)
        for name, _, tiles in P["runs"][core]:
            for slot, t in tiles:
                if t == "W":
                    v.quantize_mx(T.q[:, cols(slot)], T.s[:, cols(slot)], T.wt[:]).then_inc(T.sem[name], 1)
        for k in range(len(P["loads"][core])):
            v.wait_ge(T.sem["ld%d" % k], 16)
            for name, piece, tiles in P["runs"][core]:
                for slot, t in tiles:
                    if piece == k and t != "W":
                        r = rank[t]
                        v.quantize_mx(T.q[:, cols(slot)], T.s[:, cols(slot)],
                                      T.xt[:, 4 * TW * r:4 * TW * (r + 1)]).then_inc(T.sem[name], 1)

    sent = 0
    for level, key, waits, calls in tasks:
        for sem, count in waits:
            g.wait_ge(T.sem[sem], count if count is not None else cnt[(core, sem)])
        for call in calls:
            trs = []
            for kind, dst, a, b, n, eng, rsem in call:
                rid, pid, _ = topo.addr(dst)
                m = sum(1 << e for e in eng)
                if kind == "q":
                    src, out = T.q[:, cols(a, n)].bitcast(dt.uint8), T.q[:, cols(b, n)].bitcast(dt.uint8)
                else:
                    src, out = T.s[:, cols(a, n)], T.s[:, cols(b, n)]
                trs.append((out, src, T.sem[rsem], pid, rid, m))
                sent += len(eng)
            if len(trs) == 1:
                out, src, rs, pid, rid, m = trs[0]
                g.remote_dma(out_ap=out, in_ap=src, remote_sem=rs, local_sem=T.sem.sent, pid=pid, routing_id=rid,
                             dma_engine_mask=m)
            else:
                g.remote_dma_fused([RemoteDMATransfer(dst_ids=[DstId(rid=rid, pnc=pid)], dma_engine_mask=m,
                                                      remote_sem=rs, src=src, dst=out)
                                    for out, src, rs, pid, rid, m in trs], local_sem=T.sem.sent)
    if sent:
        g.wait_ge(T.sem.sent, sent)

    if core in rank:
        mm = sorted(P["mms"][core], key=lambda e: e[:3])
        for i, (_, w, x, waits) in enumerate(mm):
            for sem, count in waits:
                g.tensor.wait_ge(T.sem[sem], count if count is not None else cnt[(core, sem)])
            ins = g.tensor.matmul_mx(T.acc[:, 0:TW], T.q[:, cols(w)], T.s[:, cols(w)], T.q[:, cols(x)], T.s[:, cols(x)],
                                     i == 0, i == len(mm) - 1)
        ins.then_inc(T.sem.mm, 1)
        g.vector.wait_ge(T.sem.mm, 1)
        g.vector.tensor_copy(T.yo[:], T.acc[:, 0:TW]).then_inc(T.sem.cp, 1)
        g.sync.wait_ge(T.sem.cp, 1)
        g.sync.dma_start(T.y[:], T.yo[:]).then_inc(T.sem.st, 16)
        g.sync.wait_ge(T.sem.st, 16)
